import numpy as np, ml_dtypes
CORES = [48,51,52,55]
N = 4
BF = ml_dtypes.bfloat16
def gentries(a):
    return np.ascontiguousarray(a.reshape(8, 16, -1).transpose(0, 2, 1)).reshape(8, -1)
def gtable(e):
    e = np.asarray(e); return np.ascontiguousarray(e.reshape(8, -1, 16).transpose(0, 2, 1)).reshape(128, -1).astype(np.int32)
VA, G, OB, W, CAP, S = 1280, 256, 2048, 4096, 256, 272
E0, M, RO = 3, 14, 6
WA, NIL = VA + G, W - 1
H = NIL - OB
KC = 6
def within(rng, ke, k):
    o = np.argsort(ke, kind="stable"); cnt = np.bincount(ke, minlength=KC); lo = np.add.accumulate(cnt) - cnt
    i = lo[k] + (rng.random(k.shape) * np.maximum(cnt[k], 1)).astype(np.int64)
    return o[np.minimum(i, ke.size - 1)]
def feat(rng, cen, k, a):
    v = np.swapaxes(cen[np.arange(8)[None, :, None], k], 2, 3)
    return v + rng.integers(-a, a + 1, v.shape)
def parts(rng, bd=None):
    if bd is None: bd = np.argsort(rng.random((N, 8, VA)), axis=-1)[..., :G]
    cen = rng.integers(-90, 91, (8, KC, 16)); ka = rng.integers(0, KC, (N, 8, VA)); kb = rng.integers(0, KC, (N, 8, OB))
    kx = np.concatenate([ka, np.take_along_axis(np.roll(ka, 1, axis=0), np.roll(bd, 1, axis=0), 2)], axis=2)
    eo = np.argsort(kx[:, :, None, :] + 1.5 * rng.random((N, 8, 16, WA)), axis=-1); ao = np.argsort(ka[:, :, None, :] + 1.5 * rng.random((N, 8, 16, VA)), axis=-1)
    nba = np.empty((N, 8, 16, VA), np.int64); np.put_along_axis(nba, ao, eo[..., np.arange(VA) * WA // VA], -1)
    ky = np.concatenate([kb, np.roll(kb, -1, axis=0)[..., :H]], axis=2); nbb = np.empty((N, 8, 16, OB), np.int64); f0 = np.empty((N, 8, 16, S), np.int64)
    dens = rng.choice(np.array([0.3, 0.5, 0.8]), (N, 8))
    for r in range(N):
        for g in range(8):
            k = np.where(rng.random((16, OB)) < 0.75, kb[r, g], rng.integers(0, KC, (16, OB)))
            nbb[r, g] = np.where(rng.random((16, OB)) < 0.04, NIL, within(rng, ky[r, g], k))
            keep = (rng.random((16, S)) < dens[r, g]) & (rng.random((1, S)) > 0.1)
            f0[r, g] = np.where(keep, within(rng, ky[r, g], np.broadcast_to(ka[r, g, :S], (16, S))), NIL)
    return dict(cen=cen, ka=ka, kb=kb, bd=bd, nba=nba, nbb=nbb, f0=f0, xa=feat(rng, cen, ka, 3), xb=feat(rng, cen, kb, 3))
def pack(d):
    t = lambda v, w: np.ascontiguousarray(np.reshape(v, (N, 128, w)))
    return {"xa": t(d["xa"], VA).astype(np.float32).astype(BF), "xb": t(d["xb"], OB).astype(np.float32).astype(BF), "nba": t(d["nba"], VA).astype(np.int32),
            "nbb": t(d["nbb"], OB).astype(np.int32), "f0": t(d["f0"], S).astype(np.int32), "bd": np.stack([gtable(a) for a in d["bd"]])}
def put(row, c, v):
    o = np.setdiff1d(np.arange(row.size), c); hit = o[np.isin(row[o], v)]
    row[hit] = np.setdiff1d(row[c], v)[:hit.size]; row[c] = v
def short(rng, d, r, g):
    z1, z2, x = S, S + 1, VA - 1; P = np.array([S // 4, S // 2, 3 * S // 4, VA - 4, VA - 3, VA - 2])
    T = rng.permutation(np.setdiff1d(np.arange(S), P[:3])); D1, D2 = int(T[0]), int(T[1]); T = T[2:]
    f = d["f0"][r, g]; f[:] = rng.integers(0, NIL, f.shape); f[:, P[:3]] = NIL; f[:15, D1] = NIL; f[:15, D2] = NIL
    m = np.concatenate([P[:3], np.arange(S + 2, VA)])
    for p in range(16):
        c, v = [z1, z2], [D1, D2]
        if p == 0: c, v = [z1, z2, x], [x, z1, int(T[0])]
        elif p == 1: v = [z2, D2]
        elif p == 2: c, v = [z1, z2, x], [D1, D2, z1]
        elif p < 9: c, v = [z1, z2, int(P[p - 3])], [D1, D2, z2]
        elif p < 15:
            i = m[(p - 9) * T.size:(p - 8) * T.size]; c, v = np.concatenate([c, i]), np.concatenate([v, T[:i.size]])
        else: v = [z1, z2]
        put(d["nba"][r, g, p], np.array(c, np.int64), np.array(v, np.int64))
def lone(rng, d, r, g, z0, L):
    c, u, w = OB - 1, VA - 1, S
    f = d["f0"][r, g]; nb = d["nba"][r, g]; v = rng.integers(0, NIL - 1, S)
    f[:] = NIL; f[rng.integers(0, 16, S), np.arange(S)] = v + (v >= c); f[:, 64 + rng.permutation(S - 64)[:z0]] = NIL
    f[:, 0] = NIL; f[0, 0] = NIL - 1; f[1:3, 1] = c
    cells = [0, u, w] if L == 0 else [u, u - 1] + [S + i for i in range(L)]
    d["xa"][r, g][:, cells] = 40; d["xb"][r, g][:, c] = 40; d["nbb"][r, g][:, c] = c
    for p in range(16):
        if L == 0:
            to = {u: p}
            if p == 1: to[w] = u
            if p == 2: to[0] = 1
            if p == 3: to[0] = w
        else:
            to = {u: 1 if p == 1 else S, u - 1: S if p == 1 else (1 if p == 2 else p)}
            for i in range(1, L + 1): to[S + i - 1] = u if p == 4 + i else (S + i if p == 3 and i < L else 16 * i + p)
        k = sorted(to); put(nb[p], np.array(k, np.int64), np.array([to[i] for i in k], np.int64))
def quiet(rng, d, r):
    for g in range(8):
        o = rng.permutation(min(S, CAP)); x, y = int(o[0]), int(o[1]); z = int(rng.integers(2 * CAP + 1, VA)); c = int(rng.integers(0, OB))
        d["f0"][r, g] = NIL; d["f0"][r, g][:, y] = c
        for p in range(16):
            d["nba"][r, g, p] = rng.permutation(VA)
            if p == 0: k, v = [x, y], [y, x]
            else: k, v = [x, z, y], [x, y, z]
            put(d["nba"][r, g, p], np.array(k, np.int64), np.array(v, np.int64))
        b = d["xb"][r, g][:, c]; d["xa"][r, g][:, x] = b + (E0 if g < 7 else E0 + 1); d["xa"][r, g][:, z] = b - (E0 + 1)
def setup_inputs(rng):
    return pack(parts(rng))
def setup_inputs_room(rng):
    d = parts(rng); d["xa"] = feat(rng, d["cen"], d["ka"], 1); d["xb"] = feat(rng, d["cen"], d["kb"], 1); z0 = (S - VA) % CAP
    d["xa"][:, ::2, M - 1:] = 127; d["xb"][:, ::2, M - 1:] = -127; d["xa"][:, 1::2, M:] = 127; d["xb"][:, 1::2, M:] = -127
    d["xa"][:, 1::4, :M] = rng.integers(-1, 2, (N, 2, M, VA)); d["xb"][:, 1::4, :M] = rng.integers(-1, 2, (N, 2, M, OB))
    for r in range(N):
        for g in (0, 4):
            z = z0 + (0, 1, -1)[(r + g // 2) % 3]; o = rng.permutation(S)
            d["f0"][r, g][:, o[:z]] = NIL; d["f0"][r, g, rng.integers(0, 16, S - z), o[z:]] = rng.integers(0, NIL, S - z)
        lone(rng, d, r, 2, z0, 0); lone(rng, d, r, 6, z0, RO - (VA - S + z0) // CAP)
        for g in (1, 5): short(rng, d, r, g)
    return pack(d)
def setup_inputs_ties(rng):
    d = parts(rng); d["xb"] = feat(rng, d["cen"], d["kb"], 0); v = feat(rng, d["cen"], d["ka"], 0)
    d["xa"] = v + rng.choice(np.array([0, E0, E0 + 1, E0 + 2]), v.shape, p=[0.3, 0.55, 0.12, 0.03]) * rng.choice(np.array([-1, 1]), v.shape)
    d["f0"][:, ::2] = d["f0"][:, ::2, :1].copy(); d["nbb"][:, 1::2] = d["nbb"][:, 1::2, 5:6].copy(); d["nbb"][:, 0, 15] = np.arange(OB)
    quiet(rng, d, 0)
    return pack(d)
def setup_inputs_ends(rng):
    o = 1 + np.argsort(rng.random((N, 8, VA - 2)), axis=-1)[..., :G - 2]; z = np.zeros((N, 8, 1), np.int64)
    d = parts(rng, np.concatenate([z, o, z + VA - 1], axis=2)); ends = np.array([0, H - 1, H, OB - 1, OB, W - 2, NIL])
    d["cen"][::2] = d["cen"][::2, :1].copy(); d["cen"][4] = 125; d["cen"][6] = -125
    d["xa"] = feat(rng, d["cen"], d["ka"], 2); d["xb"] = feat(rng, d["cen"], d["kb"], 2)
    d["f0"] = np.where(rng.random(d["f0"].shape) < 0.5, rng.choice(ends, d["f0"].shape), d["f0"])
    e = d["nbb"][:, ::2]; d["nbb"][:, ::2] = np.where(rng.random(e.shape) < 0.5, rng.choice(ends, e.shape), e)
    d["nbb"][:, 5] = NIL; d["f0"][0, 7] = NIL; d["nba"][:, 2, 0] = np.arange(VA); d["nba"][:, 2, 1] = WA - 1 - np.arange(VA)
    return pack(d)
def setup_inputs_cross(rng):
    h = min(S, G) // 2; a = np.argsort(rng.random((N, 8, S)), axis=-1)[..., :h]; b = S + np.argsort(rng.random((N, 8, VA - S)), axis=-1)[..., :G - h]
    bd = np.concatenate([a, b], axis=2); bd = np.take_along_axis(bd, np.argsort(rng.random(bd.shape), axis=-1), 2); d = parts(rng, bd)
    noise = np.full((1, 8, 1, 1), 3); noise[:, :2] = 1; d["xa"] = feat(rng, d["cen"], d["ka"], noise); d["xb"] = feat(rng, d["cen"], d["kb"], noise)
    for r in range(N):
        for g in range(8):
            far = OB + within(rng, d["kb"][(r + 1) % N, g, :H], np.broadcast_to(d["ka"][r, g, :S], (16, S))); f = d["f0"][r, g]
            d["f0"][r, g] = np.where((f != NIL) & (rng.random(f.shape) < 0.8), far, f)
    d["f0"][1::2, :4] = NIL; lo = np.arange(VA) < CAP
    for r in range(1, N, 2):
        for g in (0, 1):
            for p in range(16):
                row = d["nba"][r, g, p]; gh = row >= VA
                i = np.flatnonzero(gh & (lo == (g == 0))); j = np.flatnonzero(~gh & (lo == (g == 1))); k = min(i.size, j.size); i = i[:k]; j = j[:k]
                vi = row[i].copy(); row[i] = row[j]; row[j] = vi
    return pack(d)
def setup_inputs_spread(rng):
    d = parts(rng); cen = rng.integers(-127, 128, (8, KC, 16))
    for x, k, n in (("xa", d["ka"], VA), ("xb", d["kb"], OB)):
        v = np.clip(feat(rng, cen, k, rng.choice(np.array([0, 1, 2, 2, 3, 3, 5, 12]), (N, 8, 1, n))), -127, 127)
        v = np.where(rng.random((N, 8, 1, n)) < 0.125, rng.integers(-127, 128, v.shape), v)
        d[x] = v * (rng.random((N, 8, 1, n)) > 0.0625)
    d["nba"][:, :, 4:8] = np.argsort(rng.random((N, 8, 4, WA)), axis=-1)[..., :VA]
    d["nbb"] = np.where(rng.random(d["nbb"].shape) < 0.3, rng.integers(0, W, d["nbb"].shape), d["nbb"])
    return pack(d)
def check_inputs(d):
    bad = []
    for k, hi in (("nba", WA - 1), ("nbb", NIL), ("f0", NIL), ("bd", VA - 1)):
        if np.min(d[k]) < 0 or np.max(d[k]) > hi: bad.append("range of " + k)
    for k in ("xa", "xb"):
        v = d[k].astype(np.float32)
        if not np.all((v >= -127) & (v <= 127) & (np.rint(v) == v)): bad.append("whole numbers of " + k)
    s = np.sort(d["nba"], axis=2)
    if np.any(s[..., 1:] == s[..., :-1]): bad.append("repeated in a row of nba")
    s = np.sort(np.stack([gentries(a) for a in d["bd"]]), axis=2)
    if np.any(s[..., 1:] == s[..., :-1]): bad.append("repeated in bd")
    return bad
def reference(xa, xb, nba, nbb, f0, bd):
    A = xa.astype(np.float32).astype(np.int32).reshape(N, 8, 16, VA); own = xb.astype(np.float32).astype(np.int32).reshape(N, 8, 16, OB)
    na = nba.astype(np.int64).reshape(N, 8, 16, VA); no = nbb.astype(np.int64).reshape(N, 8, 16, OB); bl = np.stack([gentries(a) for a in bd]).astype(np.int64)
    B = np.zeros((N, 8, 16, W), np.int32); NB = np.full((N, 8, 16, W), NIL, np.int64)
    for r in range(N):
        q = (r + 1) % N; n = no[q, :, :, :H]
        B[r, :, :, :OB] = own[r]; B[r, :, :, OB:NIL] = own[q, :, :, :H]
        NB[r, :, :, :OB] = no[r]; NB[r, :, :, OB:NIL] = np.where(n < H, OB + n, NIL)
    F = np.full((N, 8, 16, VA), NIL, np.int64); F[..., :S] = f0.reshape(N, 8, 16, S)
    flag = np.ones((N, 8, VA), bool); e = [E0] * N; rows = np.arange(16)[:, None]
    for wave in range(RO):
        ext = []
        for r in range(N):
            q = (r - 1) % N; n = np.take_along_axis(F[q], bl[q][:, None, :], 2)
            ext.append(np.concatenate([F[r], np.where((n >= OB) & (n < NIL), n - OB, NIL)], axis=2))
        for r in range(N):
            good = 0
            for g in range(8):
                a = np.flatnonzero(flag[r, g] & np.all(F[r, g] == NIL, axis=0))[:CAP]
                x = A[r, g][:, a]; c = ext[r][g][rows, na[r, g][:, a]]; col = np.arange(a.size)
                new = np.full(c.shape, NIL, np.int64)
                for t in range(3):
                    near = (np.abs(B[r, g][:, c] - x[:, None, :]) <= e[r]).astype(np.int32)
                    v = (c != NIL) & (np.add.reduce(near, axis=0) >= M); new = np.where(v, c, new); some = np.any(v, axis=0)
                    if t == 0:
                        ok = some; b = np.where(ok, c[np.argmax(v, axis=0), col], NIL)
                    else:
                        b = np.where(some, c[15 - np.argmax(v[::-1], axis=0), col], b)
                    c = NB[r, g][:, b]
                s = a[ok]; b = b[ok]; F[r, g][:, s] = new[:, ok]
                A[r, g][:, s] = x[:, ok] + np.clip(B[r, g][:, b] - x[:, ok], -2, 2)
                flag[r, g, a] = False
                w = na[r, g][:, s].reshape(-1); flag[r, g, w[w < VA]] = True
                good += int(s.size)
            e[r] = E0 + (good & 1)
    return {"yf": F.reshape(N, 128, VA).astype(np.float32), "ya": A.reshape(N, 128, VA).astype(np.float32).astype(BF)}

@@ -1,0 +1,464 @@
+from concourse.mybir import AluOpType as OPS, ActivationFunctionType as AFT, AxisListType
+
+VA, OB, CAP, S, RO = 1280, 2048, 256, 272, 6
+CH, SUB = 128, 64
+OFF = 7
+HALO = OB + 1 + OFF
+NH = 2047
+C4 = 1.5 * 2.0 ** 26
+C3 = C4 + 8.0
+
+DTS = {"b": "bfloat16", "f": "float32", "h": "float16", "i": "int32", "u": "uint16"}
+BUFS = """AW3584b BW4104b NW4104i NT2048i HN2047i NA1792i F1792f FI272i BDI16i BDU16u IND272b FL3584f EW3584f FR2560f
+IDT1280f PAD256f TN80f FC80f ECW80f EL80f CU80f WT80f PP80f OFS80f OU80u ZZ80f FH256h FRL16u FRF16f NAU256u Ch256h Th256h
+LP256h LU256u SG4096h CB256f CL256u XR4096b D4096b NE4096b VV256b SC256h Ra256f Rb256f Rc256f TI16i TM16i TX16i TU16i
+OLD16i UL16u FA16h LS16f LSU16u ES1f EI1i EO1i EC1f DX256b DC256b XN256b CI256i CJ256i GS256h YW1792f YT1280i IP1i LPI1i
+GPI1i PCF1f LPC1f GPC1f QE1f LM128f GM128f CM128f SAM128b SGL128b IDM128f IDH128h IDL128b TRI128f LTM128f WK128f TF128b
+TL128b BQ128b BC128b ONE128b OH128h XL240f HE8f GE8f ZT240f ZM1920h EPM2048b ELM2048h DPM2048h KA128f KB128f KC256f"""
+SCRATCH = {}
+for _b in BUFS.split():
+    _n = _b.rstrip("bfhiu").rstrip("0123456789")
+    SCRATCH[_n] = ("sbuf", [128, int(_b[len(_n):-1])], DTS[_b[-1]])
+for _w in range(RO):
+    SCRATCH["LG%d" % _w] = ("sbuf", [128, 256], "float16")
+PS = ("PC0", "PC1", "PQ0", "PQ1", "PT", "LPS", "LQ", "PM")
+for _n in PS:
+    SCRATCH[_n] = ("psum", [128, 512], "float32")
+LOADS = ["f0", "nba", "xa", "xb", "bd", "nbb"]
+SEMAPHORES = (["cv", "cs", "cp", "cg", "hb", "hn", "lhb", "lhn", "oy", "oa"] + ["ld_" + n for n in LOADS]
+              + [k + str(w) for k in ("gh", "lg", "xf", "xe") for w in range(RO)])
+
+
+def rank_program(g, core, T, topo):
+    rank = T.rank_of(core)
+    if rank is None:
+        return
+    nxt, prv = T.cores[(rank + 1) % 4], T.cores[(rank + 3) % 4]
+    Q = {"v": g.vector, "s": g.scalar, "p": g.tensor, "g": g, "y": g.sync}
+    CS = {"v": "cv", "s": "cs", "p": "cp", "g": "cg"}
+    cnt = {"cv": 0, "cs": 0, "cp": 0, "cg": 0}
+    known = {q: {} for q in Q}
+    clocks = {}
+    acc = {}
+
+    def need(q, sem, val):
+        if known[q].get(sem, 0) >= val:
+            return
+        Q[q].wait_ge(T.sem[sem], val)
+        known[q][sem] = val
+        for s2, v2 in clocks.get((sem, val), {}).items():
+            if known[q].get(s2, 0) < v2:
+                known[q][s2] = v2
+
+    def deps(q, reads, writes):
+        want = {}
+        for lst, isw in ((reads, False), (writes, True)):
+            for name, lo, hi in lst:
+                ps = name in PS
+                for a in acc.get(name, []):
+                    if not ps and (a[1] <= lo or hi <= a[0]):
+                        continue
+                    if ps and a[2] == q or not (isw or a[5] or ps):
+                        continue
+                    if want.get(a[3], 0) < a[4]:
+                        want[a[3]] = a[4]
+        for sem in sorted(want):
+            need(q, sem, want[sem])
+
+    def note(q, reads, writes, sem, val):
+        c = dict(known[q])
+        c[sem] = val
+        clocks[(sem, val)] = c
+        for lst, isw in ((reads, False), (writes, True)):
+            for name, lo, hi in lst:
+                l = acc.setdefault(name, [])
+                if isw or name in PS:
+                    l[:] = [a for a in l if not (name in PS or (lo <= a[0] and a[1] <= hi))]
+                else:
+                    l[:] = [a for a in l if a[5] or a[2] != q or a[3] != sem or not (lo <= a[0] and a[1] <= hi)]
+                l.append([lo, hi, q, sem, val, isw])
+
+    def A(name, lo=0, hi=None, st=1):
+        if hi is None:
+            hi = T[name].shape[1]
+        ap = T[name][:, lo:hi] if st == 1 else T[name][:, lo:hi:st]
+        return (ap, [(name, lo, hi)], [])
+
+    def I(win, w, off, o0, o1):
+        return (T[win][:, 0:w].indirect(T[off][:, o0:o1]), [(win, 0, w)], [(off, o0, o1)])
+
+    def op(q, out, ins, call):
+        reads = list(out[2])
+        for x in ins:
+            reads += x[1] + x[2]
+        deps(q, reads, out[1])
+        sem = CS[q]
+        cnt[sem] += 1
+        call().then_inc(T.sem[sem], 1)
+        note(q, reads, out[1], sem, cnt[sem])
+
+    def u(x):
+        return x[0] if isinstance(x, tuple) else x
+
+    def cp(out, in_):
+        op("v", out, [in_], lambda: g.vector.tensor_copy(out=out[0], in_=in_[0]))
+
+    def tt(out, a, b, o):
+        op("v", out, [a, b], lambda: g.vector.tensor_tensor(out=out[0], in0=a[0], in1=b[0], op=o))
+
+    def ts(out, a, s1, o0, s2=None, o1=None):
+        ins = [a] + [x for x in (s1, s2) if isinstance(x, tuple)]
+        if o1 is None:
+            op("v", out, ins, lambda: g.vector.tensor_scalar(out=out[0], in0=a[0], scalar1=u(s1), scalar2=None, op0=o0))
+        else:
+            op("v", out, ins, lambda: g.vector.tensor_scalar(out=out[0], in0=a[0], scalar1=u(s1), scalar2=u(s2), op0=o0, op1=o1))
+
+    def ms(out, c):
+        op("v", out, [], lambda: g.vector.memset(out[0], c))
+
+    def act(out, in_, f=AFT.Copy, bias=0.0, scale=1.0):
+        if bias == 0.0 and scale == 1.0:
+            op("s", out, [in_], lambda: g.scalar.activation(out=out[0], in_=in_[0], func=f))
+        else:
+            op("s", out, [in_], lambda: g.scalar.activation(out=out[0], in_=in_[0], func=f, bias=bias, scale=scale))
+
+    def mm(out, lhsT, rhs, st, sp):
+        op("p", out, [lhsT, rhs], lambda: g.tensor.matmul(out=out[0], lhsT=lhsT[0], rhs=rhs[0], start=st, stop=sp))
+
+    def io(out, pat, base, cm=0, small=True):
+        if small:
+            op("g", out, [], lambda: g.iota(out[0], pat, base, cm, allow_small_or_imprecise_dtypes=True))
+        else:
+            op("g", out, [], lambda: g.iota(out[0], pat, base, cm))
+
+    def dma(q, out_ap, in_ap, reads, writes, sem):
+        deps(q, reads, writes)
+        Q[q].dma_start(out=out_ap, in_=in_ap).then_inc(T.sem[sem], 16)
+        note(q, reads, writes, sem, 16)
+
+    def send(dst, outp, inp, rsem, lsem):
+        deps("g", inp[1], [])
+        rid, pid, _ = topo.addr(dst)
+        g.remote_dma(out_ap=outp[0], in_ap=inp[0], remote_sem=T.sem[rsem], local_sem=T.sem[lsem], pid=pid, routing_id=rid,
+                     dma_engine_mask=topo.mask(core, dst))
+        note("g", inp[1], [], lsem, len(topo.engines(core, dst)))
+
+    def arrive(src, outp, rsem):
+        acc.setdefault(outp[1][0][0], []).append([outp[1][0][1], outp[1][0][2], "r", rsem, len(topo.engines(src, core)), True])
+
+    dma("y", T.FI[:], T.f0[:], [], [("FI", 0, S)], "ld_f0")
+    dma("s", T.BW[:, 8:8 + OB], T.xb[:], [], [("BW", 8, 8 + OB)], "ld_xb")
+    dma("y", T.NA[:, 0:VA], T.nba[:], [], [("NA", 0, VA)], "ld_nba")
+    dma("s", T.AW[:, 0:VA], T.xa[:], [], [("AW", 0, VA)], "ld_xa")
+    dma("y", T.BDI[:], T.bd[:], [], [("BDI", 0, 16)], "ld_bd")
+    dma("y", T.NT[:], T.nbb[:], [], [("NT", 0, OB)], "ld_nbb")
+    HB, HNB = A("BW", HALO, HALO + NH), A("NW", HALO, HALO + NH)
+    arrive(nxt, HB, "hb")
+    arrive(nxt, HNB, "hn")
+    for w in range(RO):
+        arrive(prv, A("LG%d" % w), "gh%d" % w)
+
+    io(A("IP"), [[0, 1]], 0, 1, False)
+    io(A("LM"), [[0, 8], [1, 16]], 1)
+    io(A("GM"), [[1, 8], [0, 16]], 0)
+    io(A("CM"), [[1, 128]], 0)
+    io(A("TN"), [[1, 80]], VA)
+    io(A("PAD"), [[1, CAP]], 1536 + 64)
+    io(A("IDT"), [[1, 80], [80, 16]], 64)
+    io(A("NA", VA, 1792), [[1, 512]], VA, 0, False)
+    io(A("XL"), [[1, 240]], -112)
+    io(A("HE"), [[1, 8]], 0)
+    send(prv, HB, A("BW", 8, 8 + NH), "hb", "lhb")
+    ms(A("FL", 0, VA), 33.0)
+    ms(A("EW", S, VA), 0.0)
+    ms(A("F", S, 1792), 0.0)
+    ms(A("ZZ"), 0.0)
+    ms(A("KB"), 64.0)
+    ms(A("KA"), 33.0)
+    ms(A("KC"), 0.0)
+    ts(A("LPI"), A("IP"), 15, OPS.bitwise_and)
+    ts(A("GPI"), A("IP"), 4, OPS.arith_shift_right)
+    cp(A("PCF"), A("IP"))
+    ts(A("LPC"), A("LPI"), 1.0, OPS.add)
+    cp(A("GPC"), A("GPI"))
+    ts(A("QE"), A("LPI"), 80.0, OPS.mult)
+    ts(A("TN"), A("TN"), A("QE"), OPS.add)
+    ts(A("SAM"), A("GM"), A("GPC"), OPS.is_equal)
+    ts(A("FI"), A("FI"), 1.0, OPS.add)
+    ts(A("IDM"), A("CM"), A("PCF"), OPS.is_equal)
+    ts(A("FI"), A("FI"), 4095, OPS.bitwise_and)
+    ts(A("WK"), A("LM"), A("LPC"), OPS.is_gt)
+    cp(A("F", 0, S), A("FI"))
+    tt(A("TRI"), A("WK"), A("SAM"), OPS.mult)
+    ts(A("IND"), A("F", 0, S), 0.0, OPS.is_gt)
+    mm(A("PM", 0, S), A("SAM"), A("IND"), True, True)
+    cp(A("BDU"), A("BDI"))
+    tt(A("IDL"), A("IDM"), A("LM"), OPS.mult)
+    ts(A("EW", 0, S), A("PM", 0, S), 0.5, OPS.is_gt, 64.0, OPS.mult)
+
+    def ghosts_out(w):
+        ts(A("GS"), I("F", VA, "BDU", 0, 16), 2048.0, OPS.subtract, 0.0, OPS.max)
+        send(nxt, A("LG%d" % w), A("GS"), "gh%d" % w, "lg%d" % w)
+
+    def extract(w):
+        dma("y", T.ECW[:], T.EW[0:128:16, 0:VA], [("EW", 0, VA)], [("ECW", 0, 80)], "xe%d" % w)
+        dma("y", T.FC[:], T.FL[0:128:16, 0:VA], [("FL", 0, VA)], [("FC", 0, 80)], "xf%d" % w)
+
+    def select_a(w):
+        tt(A("EL"), A("FC"), A("ECW"), OPS.is_gt)
+        op("v", A("CU"), [A("EL"), A("ZZ")], lambda: g.vector.tensor_tensor_scan(
+            out=T.CU[:], data0=T.EL[:], data1=T.ZZ[:], initial=0.0, op0=OPS.add, op1=OPS.add))
+        mm(A("PM", 0, 1), A("TRI"), A("CU", 79, 80), True, True)
+        ts(A("WT"), A("EL"), -4096.0, OPS.mult)
+        tt(A("WT"), A("WT"), A("TN"), OPS.add)
+        ts(A("PP"), A("CU"), A("PM", 0, 1), OPS.add, 1.0, OPS.subtract)
+        tt(A("OFS"), A("WT"), A("PP"), OPS.max)
+        cp(A("OU"), A("OFS"))
+        act(A("FR", 0, CAP), A("PAD"))
+        act(I("FR", 2560, "OU", 0, 80), A("IDT"), AFT.Silu)
+
+    def select_b():
+        cp(A("FH"), A("FR", 0, CAP))
+        for l in range(16):
+            mm(A("PM", 16, 32), A("DPM", 128 * l, 128 * l + 128), A("FH", l, CAP, 16), l == 0, l == 15)
+        ts(A("FRL"), A("PM", 16, 32), 64.0, OPS.subtract)
+        cp(A("NAU"), I("NA", 1792, "FRL", 0, 16))
+        ts(A("FRF"), A("PM", 16, 32), 64.0, OPS.subtract)
+
+    extract(0)
+    ghosts_out(0)
+    for p in range(16):
+        ts(A("DPM", 128 * p, 128 * p + 128), A("IDL"), float(p + 1), OPS.is_equal)
+    select_a(0)
+    tt(A("SGL"), A("SAM"), A("LM"), OPS.mult)
+    ms(A("BW", 0, 8), 1024.0)
+    ms(A("NW", 0, 8), 0)
+    ms(A("AW", VA, 1792), 0.0)
+    ms(A("EC"), C3)
+    for p in range(16):
+        ts(A("EPM", 128 * p, 128 * p + 128), A("SGL"), float(p + 1), OPS.is_equal, 1024.0, OPS.mult)
+    ms(A("BC"), -109.0)
+    ms(A("BQ"), -4.0)
+    ms(A("ONE"), 1.0)
+    ts(A("WK"), A("LM"), A("LPC"), OPS.is_lt)
+    tt(A("LTM"), A("WK"), A("SAM"), OPS.mult)
+    for m, o in (("TRI", "TF"), ("LTM", "TL")):
+        tt(A("WK"), A("IDM"), A(m), OPS.subtract)
+        ts(A(o), A("WK"), 1024.0, OPS.mult)
+    for p in range(16):
+        ts(A("ELM", 128 * p, 128 * p + 128), A("SGL"), float(p + 1), OPS.is_equal, 16.0, OPS.mult)
+    ts(A("OH"), A("ONE"), 1.0 / 256.0, OPS.mult)
+    cp(A("IDH"), A("IDM"))
+    ts(A("ZT"), A("XL"), 1.0, OPS.add, A("LPC"), OPS.is_equal)
+    ts(A("GE"), A("HE"), A("GPC"), OPS.is_equal)
+    for h in range(8):
+        ts(A("ZM", 240 * h, 240 * h + 240), A("ZT"), A("GE", h, h + 1), OPS.mult)
+    select_b()
+
+    def pc(X, lo, hi):
+        return A("PC%d" % X, lo, hi)
+
+    def seeds(q, X, s):
+        a = CH * X + SUB * s
+        if q == "v":
+            ts(A("SG", 16 * a, 16 * a + 1024), I("F", 1792, "NAU", a, a + SUB), 2048.0, OPS.subtract, 0.0625, OPS.mult)
+        else:
+            act(A("SG", 16 * a, 16 * a + 1024), I("F", 1792, "NAU", a, a + SUB), AFT.Copy, -128.0, 0.0625)
+        for p in range(16):
+            mm(pc(X, SUB * s, SUB * s + SUB), A("DPM", 128 * p, 128 * p + 128), A("SG", 16 * a + p, 16 * a + 1024, 16), p == 0, p == 15)
+
+    def slist(X):
+        ts(A("CL", CH * X, CH * X + CH), pc(X, 0, CH), 16.0, OPS.mult, 2048.0 + OFF, OPS.add)
+        act(A("CB", CH * X, CH * X + CH), pc(X, 0, CH))
+
+    def xrep(q, X):
+        f = cp if q == "v" else act
+        a, b = 16 * CH * X, 16 * CH * X + 16 * CH
+        f(A("XR", a, b, 16), I("AW", 1792, "FRL", 8 * X, 8 * X + 8))
+        for k in (8, 4, 2, 1):
+            f(A("XR", a + k, b, 2 * k), A("XR", a, b, 2 * k))
+
+    def G(X, s):
+        a = CH * X + SUB * s
+        tt(A("D", 16 * a, 16 * a + 1024), I("BW", HALO + NH, "CL", a, a + SUB), A("XR", 16 * a, 16 * a + 1024), OPS.subtract)
+
+    def H(X, s):
+        a = CH * X + SUB * s
+        ts(A("NE", 16 * a, 16 * a + 1024), A("D", 16 * a, 16 * a + 1024), A("EC"), OPS.add, A("EC"), OPS.is_equal)
+        for p in range(16):
+            mm(pc(X, SUB * s, SUB * s + SUB), A("EPM", 128 * p, 128 * p + 128), A("NE", 16 * a + p, 16 * a + 1024, 16), p == 0, False)
+        mm(pc(X, SUB * s, SUB * s + SUB), A("BC"), A("ONE", 0, SUB), False, True)
+
+    def o1(t, X):
+        a = CH * X
+        ts(A("VV", a, a + CH), pc(X, 0, CH), 0.0, OPS.is_ge)
+        mm(A("PQ%d" % X, 0, CH), A("TF" if t == 0 else "TL"), A("VV", a, a + CH), True, False)
+        mm(A("PQ%d" % X, 0, CH), A("BQ"), A("ONE"), False, True)
+
+    def o5(t, X):
+        a = CH * X
+        tt(A("SC", a, a + CH), A("PQ%d" % X, 0, CH), A("CB", a, a + CH), OPS.min)
+        for l in range(16):
+            mm(A("PQ%d" % X, 128, 136), A("ELM", 128 * l, 128 * l + 128), A("SC", a + l, a + CH, 16), l == 0, l == 15)
+
+    def tiny(t, X):
+        lo, hi = 8 * X, 8 * X + 8
+        ts(A("TI", lo, hi), A("PQ%d" % X, 128, 136), 2048.0, OPS.add)
+        ts(A("TM", lo, hi), A("TI", lo, hi), 16383, OPS.bitwise_and)
+        if t == 0:
+            ts(A("TX", lo, hi), A("TM", lo, hi), 4096.0, OPS.max)
+        else:
+            tt(A("TX", lo, hi), A("TM", lo, hi), A("OLD", lo, hi), OPS.max)
+        ts(A("TU", lo, hi), A("TX", lo, hi), 4095, OPS.bitwise_and)
+        ts(A("UL", lo, hi), A("TU", lo, hi), float(OFF), OPS.add)
+        if t < 2:
+            ts(A("OLD", lo, hi), A("TU", lo, hi), 4096.0, OPS.add)
+
+    def fails(w, X):
+        lo, hi, a = 8 * X, 8 * X + 8, CH * X
+        ts(A("FA", lo, hi), A("TM", lo, hi), 8192.0, OPS.is_lt, 1792.0, OPS.mult)
+        tt(A("LS", lo, hi), A("FRF", lo, hi), A("FA", lo, hi), OPS.add)
+        cp(A("LSU", lo, hi), A("LS", lo, hi))
+        if w == RO - 1:
+            return
+        mm(A("LQ", a, a + CH), A("IDH"), A("LP", a, a + CH), True, False)
+        for p in range(16):
+            mm(A("LQ", a + 8 * p, a + 8 * p + 8), A("IDH"), A("FA", lo, hi), False, p == 15)
+        cp(A("LU", a, a + CH), A("LQ", a, a + CH))
+        act(I("EW", 3584, "LSU", lo, hi), A("KB"), AFT.Silu)
+        for p in range(16):
+            act(I("FL", 3584, "LU", a + 8 * p, a + 8 * p + 8), A("KA"), AFT.Silu)
+
+    def nbg(X):
+        a = CH * X
+        ts(A("CB", a, a + CH), I("NW", HALO + NH, "UL", 8 * X, 8 * X + 8), 2048.0, OPS.subtract, 0.0625, OPS.mult)
+        ts(A("CL", a, a + CH), A("CB", a, a + CH), 16.0, OPS.mult, 2048.0 + OFF, OPS.add)
+
+    RN = ("Ra", "Rb", "Rc")
+
+    def rt(t, X):
+        a = CH * X
+        tt(A(RN[t], a, a + CH), pc(X, 0, CH), A("CB", a, a + CH), OPS.min)
+
+    def relay_a():
+        cp(A("Ch"), A("NAU"))
+        for h in range(2):
+            for k in range(8):
+                mm(A("PT", 32 * k + 16 * h, 32 * k + 16 * h + 16), A("Ch", 128 * h, 128 * h + 128), A("IDH", 16 * k, 16 * k + 16), True, True)
+        cp(A("Th"), A("PT", 0, 256))
+
+    def relay_b():
+        for h in range(8):
+            for k in range(8):
+                mm(A("LPS", h, 256, 8), A("ZM", 240 * h + 112 - 16 * k, 240 * h + 240 - 16 * k), A("Th", 32 * k, 32 * k + 32), k == 0, k == 7)
+
+    def merge01():
+        ts(A("Ra"), A("Ra"), 512.0, OPS.subtract)
+        ts(A("Rb"), A("Rb"), 256.0, OPS.subtract)
+        tt(A("Ra"), A("Ra"), A("Rb"), OPS.max)
+
+    def decode(w, X):
+        a, b = CH * X, CH * X + CH
+        rt(2, X)
+        tt(A("Rc", a, b), A("Rc", a, b), A("Ra", a, b), OPS.max)
+        ts(A("CI", a, b), A("Rc", a, b), 16.0, OPS.mult, 2048.0, OPS.add)
+        ts(A("CJ", a, b), A("CI", a, b), 4095, OPS.bitwise_and)
+        if w < RO - 1:
+            cp(I("F", 1792, "FRL", 8 * X, 8 * X + 8), A("CJ", a, b))
+        else:
+            ts(A("CI", a, b), A("CJ", a, b), 1.0, OPS.subtract)
+            ts(A("CJ", a, b), A("CI", a, b), 4095, OPS.bitwise_and)
+            cp(I("YW", 1792, "FRL", 8 * X, 8 * X + 8), A("CJ", a, b))
+
+    def update_a():
+        xs = A("XR", 0, 4096, 16)
+        tt(A("DX"), I("BW", HALO + NH, "UL", 0, 16), xs, OPS.subtract)
+        ts(A("DC"), A("DX"), -2.0, OPS.max, 2.0, OPS.min)
+        tt(A("XN"), A("DC"), xs, OPS.add)
+        cp(I("AW", 3584, "LSU", 0, 16), A("XN"))
+
+    def parity():
+        mm(A("PM", 64, 80), A("OH"), A("FA"), True, True)
+        op("v", A("ES"), [A("PM", 64, 80)], lambda: g.vector.tensor_reduce(out=T.ES[:], in_=T.PM[:, 64:80], axis=AxisListType.X, op=OPS.add))
+        cp(A("EI"), A("ES"))
+        ts(A("EO"), A("EI"), 1, OPS.bitwise_and)
+        ts(A("EC"), A("EO"), -8.0, OPS.mult, C3, OPS.add)
+
+    for w in range(RO):
+        last = w == RO - 1
+        cp(A("F", VA, VA + 256), A("LG%d" % w))
+        seeds("v", 0, 0)
+        seeds("s", 0, 1)
+        seeds("v", 1, 0)
+        seeds("s", 1, 1)
+        if not last:
+            relay_a()
+        xrep("v", 0)
+        slist(0)
+        xrep("s", 1)
+        if not last:
+            act(I("FL", 3584, "FRL", 0, 16), A("KC"), AFT.Silu)
+            relay_b()
+        G(0, 0)
+        slist(1)
+        G(0, 1)
+        H(0, 0)
+        H(0, 1)
+        if not last:
+            cp(A("LP"), A("LPS", 0, 256))
+        if w == 0:
+            ts(A("NW", 8, 8 + OB), A("NT"), 1.0, OPS.add)
+            ts(A("HN"), A("NT", 0, NH), 2047.0, OPS.min, 2049.0, OPS.add)
+            ts(A("HN"), A("HN"), 4095, OPS.bitwise_and)
+            send(prv, HNB, A("HN"), "hn", "lhn")
+            ts(A("NW", 8, 8 + OB), A("NW", 8, 8 + OB), 4095, OPS.bitwise_and)
+        for t in range(3):
+            for X in range(2):
+                if t == 2 and X == 1:
+                    break
+                nX = 1 - X
+                G(nX, 0)
+                o1(t, X)
+                G(nX, 1)
+                o5(t, X)
+                H(nX, 0)
+                H(nX, 1)
+                tiny(t, X)
+                if t < 2:
+                    rt(t, X)
+                    nbg(X)
+                if t == 0:
+                    fails(w, X)
+        merge01()
+        decode(w, 0)
+        if not last:
+            extract(w + 1)
+        decode(w, 1)
+        if not last:
+            ghosts_out(w + 1)
+            select_a(w + 1)
+        else:
+            dma("y", T.yf[:], T.YW[:, 0:VA], [("YW", 0, VA)], [], "oy")
+        o1(2, 1)
+        o5(2, 1)
+        if not last:
+            parity()
+        tiny(2, 1)
+        update_a()
+        if last:
+            dma("y", T.ya[:], T.AW[:, 0:VA], [("AW", 0, VA)], [], "oa")
+        elif w == RO - 2:
+            ts(A("YT"), A("F", 0, VA), 1.0, OPS.subtract)
+            ts(A("YT"), A("YT"), 4095, OPS.bitwise_and)
+            cp(A("YW", 0, VA), A("YT"))
+        if not last:
+            select_b()
+
+    need("y", "oy", 16)
+    need("y", "oa", 16)
+    for w in range(RO):
+        need("g", "lg%d" % w, 16)
+    need("g", "lhb", 16)
+    need("g", "lhn", 16)
+    for s in ("cv", "cs", "cp", "cg"):
+        need("y", s, cnt[s])

@@ -9,19 +9,20 @@ C4 = 1.5 * 2.0 ** 26
 C3 = C4 + 8.0
 
 DTS = {"b": "bfloat16", "f": "float32", "h": "float16", "i": "int32", "u": "uint16"}
-BUFS = """AW3584b BW4104b NW4104i NT2048i HN2047i NA1792i F1792f FI272i BDI16i BDU16u IND272b FL3584f EW3584f FR2560f
+BUFS = """AW3584b BW4104b NW4104f NT2048i HN2047f NA1792i F1792f FI272i BDI16i BDU16u IND320b FL3584f EW3584f FR2560f
 IDT1280f PAD256f TN80f FC80f ECW80f EL80f CU80f WT80f PP80f OFS80f OU80u ZZ80f FH256h FRL16u FRF16f NAU256u Ch256h Th256h
-LP256h LU256u SG4096h CB256f CL256u XR4096b D4096b NE4096b VV256b SC256h Ra256f Rb256f Rc256f TI16i TM16i TX16i TU16i
-OLD16i UL16u FA16h LS16f LSU16u ES1f EI1i EO1i EC1f DX256b DC256b XN256b CI256i CJ256i GS256h YW1792f YT1280i IP1i LPI1i
+LP256h LU256u SG4096h CB256f CL256u XR4096b D4096b NE4096b VV256b SC256h SA256f SB256f Ra256f Rb256f Rc256f TI16i TM16i
+TU16i UL16u FA16h LS16f LSU16u ES1f EI1i EO1i EC1f DX256b DC256b CI256i CJ256i GS256h YW1792f YT1280i IP1i LPI1i
 GPI1i PCF1f LPC1f GPC1f QE1f LM128f GM128f CM128f SAM128b SGL128b IDM128f IDH128h IDL128b TRI128f LTM128f WK128f TF128b
-TL128b BQ128b BC128b ONE128b OH128h XL240f HE8f GE8f ZT240f ZM1920h EPM2048b ELM2048h DPM2048h KA128f KB128f KC256f"""
+TL128b TB128b TC128b BC128b BR128f ONE128b OH128h XL240f HE8f GE8f ZT240f ZM1920h EPM2048b ELM2048h DPM2048h KA128f
+KB256f KC256f"""
 SCRATCH = {}
 for _b in BUFS.split():
     _n = _b.rstrip("bfhiu").rstrip("0123456789")
     SCRATCH[_n] = ("sbuf", [128, int(_b[len(_n):-1])], DTS[_b[-1]])
 for _w in range(RO):
     SCRATCH["LG%d" % _w] = ("sbuf", [128, 256], "float16")
-PS = ("PC0", "PC1", "PQ0", "PQ1", "PT", "LPS", "LQ", "PM")
+PS = ("PC0", "PC1", "PQ0", "PQ1", "PR", "PM")
 for _n in PS:
     SCRATCH[_n] = ("psum", [128, 512], "float32")
 LOADS = ["f0", "nba", "xa", "xb", "bd", "nbb"]
@@ -58,7 +59,7 @@ def rank_program(g, core, T, topo):
                 for a in acc.get(name, []):
                     if not ps and (a[1] <= lo or hi <= a[0]):
                         continue
-                    if ps and a[2] == q or not (isw or a[5] or ps):
+                    if ps and a[2] == q and (q == "p" or not a[5]) or not (isw or a[5] or ps):
                         continue
                     if want.get(a[3], 0) < a[4]:
                         want[a[3]] = a[4]
@@ -131,6 +132,9 @@ def rank_program(g, core, T, topo):
         else:
             op("g", out, [], lambda: g.iota(out[0], pat, base, cm))
 
+    def gcopy(out, in_, n):
+        op("g", out, [in_], lambda: g.affine_select(out[0], in_[0], [[0, n]], OPS.is_gt, 0.0, 1, 0))
+
     def dma(q, out_ap, in_ap, reads, writes, sem):
         deps(q, reads, writes)
         Q[q].dma_start(out=out_ap, in_=in_ap).then_inc(T.sem[sem], 16)
@@ -146,12 +150,11 @@ def rank_program(g, core, T, topo):
     def arrive(src, outp, rsem):
         acc.setdefault(outp[1][0][0], []).append([outp[1][0][1], outp[1][0][2], "r", rsem, len(topo.engines(src, core)), True])
 
-    dma("y", T.FI[:], T.f0[:], [], [("FI", 0, S)], "ld_f0")
+    dma("s", T.FI[:], T.f0[:], [], [("FI", 0, S)], "ld_f0")
     dma("s", T.BW[:, 8:8 + OB], T.xb[:], [], [("BW", 8, 8 + OB)], "ld_xb")
+    dma("y", T.BDI[:], T.bd[:], [], [("BDI", 0, 16)], "ld_bd")
     dma("y", T.NA[:, 0:VA], T.nba[:], [], [("NA", 0, VA)], "ld_nba")
     dma("s", T.AW[:, 0:VA], T.xa[:], [], [("AW", 0, VA)], "ld_xa")
-    dma("y", T.BDI[:], T.bd[:], [], [("BDI", 0, 16)], "ld_bd")
-    dma("y", T.NT[:], T.nbb[:], [], [("NT", 0, OB)], "ld_nbb")
     HB, HNB = A("BW", HALO, HALO + NH), A("NW", HALO, HALO + NH)
     arrive(nxt, HB, "hb")
     arrive(nxt, HNB, "hn")
@@ -169,6 +172,8 @@ def rank_program(g, core, T, topo):
     io(A("XL"), [[1, 240]], -112)
     io(A("HE"), [[1, 8]], 0)
     send(prv, HB, A("BW", 8, 8 + NH), "hb", "lhb")
+    need("y", "lhb", len(topo.engines(core, prv)))
+    dma("y", T.NT[:], T.nbb[:], [], [("NT", 0, OB)], "ld_nbb")
     ms(A("FL", 0, VA), 33.0)
     ms(A("EW", S, VA), 0.0)
     ms(A("F", S, 1792), 0.0)
@@ -190,21 +195,24 @@ def rank_program(g, core, T, topo):
     ts(A("WK"), A("LM"), A("LPC"), OPS.is_gt)
     cp(A("F", 0, S), A("FI"))
     tt(A("TRI"), A("WK"), A("SAM"), OPS.mult)
-    ts(A("IND"), A("F", 0, S), 0.0, OPS.is_gt)
-    mm(A("PM", 0, S), A("SAM"), A("IND"), True, True)
-    cp(A("BDU"), A("BDI"))
+    ts(A("IND"), A("F", 0, 320), 0.0, OPS.is_gt)
+    tt(A("SGL"), A("SAM"), A("LM"), OPS.mult)
+    for q in range(4):
+        ts(A("EPM", 128 * q, 128 * q + 128), A("SGL"), float(q + 1), OPS.is_equal, 1024.0, OPS.mult)
+        mm(A("PM", 0, 80), A("EPM", 128 * q, 128 * q + 128), A("IND", 80 * q, 80 * q + 80), q == 0, q == 3)
+    ms(A("FC"), 33.0)
     tt(A("IDL"), A("IDM"), A("LM"), OPS.mult)
-    ts(A("EW", 0, S), A("PM", 0, S), 0.5, OPS.is_gt, 64.0, OPS.mult)
+    ts(A("ECW"), A("PM", 0, 80), 0.5, OPS.is_gt, 64.0, OPS.mult)
 
     def ghosts_out(w):
-        ts(A("GS"), I("F", VA, "BDU", 0, 16), 2048.0, OPS.subtract, 0.0, OPS.max)
+        act(A("GS"), I("F", VA, "BDU", 0, 16), AFT.Relu, -2048.0)
         send(nxt, A("LG%d" % w), A("GS"), "gh%d" % w, "lg%d" % w)
 
     def extract(w):
         dma("y", T.ECW[:], T.EW[0:128:16, 0:VA], [("EW", 0, VA)], [("ECW", 0, 80)], "xe%d" % w)
         dma("y", T.FC[:], T.FL[0:128:16, 0:VA], [("FL", 0, VA)], [("FC", 0, 80)], "xf%d" % w)
 
-    def select_a(w):
+    def select_a():
         tt(A("EL"), A("FC"), A("ECW"), OPS.is_gt)
         op("v", A("CU"), [A("EL"), A("ZZ")], lambda: g.vector.tensor_tensor_scan(
             out=T.CU[:], data0=T.EL[:], data1=T.ZZ[:], initial=0.0, op0=OPS.add, op1=OPS.add))
@@ -218,42 +226,47 @@ def rank_program(g, core, T, topo):
         act(I("FR", 2560, "OU", 0, 80), A("IDT"), AFT.Silu)
 
     def select_b():
-        cp(A("FH"), A("FR", 0, CAP))
+        act(A("FH"), A("FR", 0, CAP))
         for l in range(16):
             mm(A("PM", 16, 32), A("DPM", 128 * l, 128 * l + 128), A("FH", l, CAP, 16), l == 0, l == 15)
         ts(A("FRL"), A("PM", 16, 32), 64.0, OPS.subtract)
         cp(A("NAU"), I("NA", 1792, "FRL", 0, 16))
         ts(A("FRF"), A("PM", 16, 32), 64.0, OPS.subtract)
 
-    extract(0)
+    select_a()
+    cp(A("BDU"), A("BDI"))
     ghosts_out(0)
+    mm(A("PM", 128, 128 + S), A("SAM"), A("IND", 0, S), True, True)
+    ts(A("EW", 0, S), A("PM", 128, 128 + S), 0.5, OPS.is_gt, 64.0, OPS.mult)
     for p in range(16):
         ts(A("DPM", 128 * p, 128 * p + 128), A("IDL"), float(p + 1), OPS.is_equal)
-    select_a(0)
-    tt(A("SGL"), A("SAM"), A("LM"), OPS.mult)
     ms(A("BW", 0, 8), 1024.0)
-    ms(A("NW", 0, 8), 0)
+    ms(A("NW", 0, 8), -2048.0)
     ms(A("AW", VA, 1792), 0.0)
     ms(A("EC"), C3)
-    for p in range(16):
+    for p in range(4, 16):
         ts(A("EPM", 128 * p, 128 * p + 128), A("SGL"), float(p + 1), OPS.is_equal, 1024.0, OPS.mult)
-    ms(A("BC"), -109.0)
-    ms(A("BQ"), -4.0)
+    cp(A("IDH"), A("IDM"))
+    ts(A("BR"), A("IDM"), -128.0, OPS.mult)
     ms(A("ONE"), 1.0)
     ts(A("WK"), A("LM"), A("LPC"), OPS.is_lt)
     tt(A("LTM"), A("WK"), A("SAM"), OPS.mult)
-    for m, o in (("TRI", "TF"), ("LTM", "TL")):
+    for m, o, b in (("TRI", "TF", "TB"), ("LTM", "TL", "TC")):
         tt(A("WK"), A("IDM"), A(m), OPS.subtract)
-        ts(A(o), A("WK"), 1024.0, OPS.mult)
-    for p in range(16):
-        ts(A("ELM", 128 * p, 128 * p + 128), A("SGL"), float(p + 1), OPS.is_equal, 16.0, OPS.mult)
-    ts(A("OH"), A("ONE"), 1.0 / 256.0, OPS.mult)
-    cp(A("IDH"), A("IDM"))
-    ts(A("ZT"), A("XL"), 1.0, OPS.add, A("LPC"), OPS.is_equal)
-    ts(A("GE"), A("HE"), A("GPC"), OPS.is_equal)
-    for h in range(8):
-        ts(A("ZM", 240 * h, 240 * h + 240), A("ZT"), A("GE", h, h + 1), OPS.mult)
+        ts(A(o), A("WK"), 512.0, OPS.mult)
+        ts(A(b), A(m), -512.0, OPS.mult)
+        tt(A(b), A(b), A("BR"), OPS.add)
     select_b()
+
+    def rest():
+        for p in range(16):
+            ts(A("ELM", 128 * p, 128 * p + 128), A("SGL"), float(p + 1), OPS.is_equal, 16.0, OPS.mult)
+        ts(A("OH"), A("ONE"), 1.0 / 256.0, OPS.mult)
+        ts(A("BC"), A("ONE"), -109.0, OPS.mult)
+        ts(A("ZT"), A("XL"), 1.0, OPS.add, A("LPC"), OPS.is_equal)
+        ts(A("GE"), A("HE"), A("GPC"), OPS.is_equal)
+        for h in range(8):
+            ts(A("ZM", 240 * h, 240 * h + 240), A("ZT"), A("GE", h, h + 1), OPS.mult)
 
     def pc(X, lo, hi):
         return A("PC%d" % X, lo, hi)
@@ -271,29 +284,31 @@ def rank_program(g, core, T, topo):
         ts(A("CL", CH * X, CH * X + CH), pc(X, 0, CH), 16.0, OPS.mult, 2048.0 + OFF, OPS.add)
         act(A("CB", CH * X, CH * X + CH), pc(X, 0, CH))
 
-    def xrep(q, X):
-        f = cp if q == "v" else act
+    def xrep(X):
         a, b = 16 * CH * X, 16 * CH * X + 16 * CH
-        f(A("XR", a, b, 16), I("AW", 1792, "FRL", 8 * X, 8 * X + 8))
-        for k in (8, 4, 2, 1):
-            f(A("XR", a + k, b, 2 * k), A("XR", a, b, 2 * k))
+        (act if X else cp)(A("XR", a, b, 16), I("AW", 1792, "FRL", 8 * X, 8 * X + 8))
+        for k, n in ((8, 128), (4, 256), (2, 512), (1, 1024)):
+            if X:
+                gcopy(A("XR", a + k, b, 2 * k), A("XR", a, b, 2 * k), n)
+            else:
+                cp(A("XR", a + k, b, 2 * k), A("XR", a, b, 2 * k))
 
-    def G(X, s):
-        a = CH * X + SUB * s
-        tt(A("D", 16 * a, 16 * a + 1024), I("BW", HALO + NH, "CL", a, a + SUB), A("XR", 16 * a, 16 * a + 1024), OPS.subtract)
+    def G(X, s, n=SUB):
+        a = 16 * (CH * X + SUB * s)
+        tt(A("D", a, a + 16 * n), I("BW", 4104, "CL", a // 16, a // 16 + n), A("XR", a, a + 16 * n), OPS.subtract)
 
-    def H(X, s):
-        a = CH * X + SUB * s
-        ts(A("NE", 16 * a, 16 * a + 1024), A("D", 16 * a, 16 * a + 1024), A("EC"), OPS.add, A("EC"), OPS.is_equal)
+    def H(X, s, n=SUB):
+        a, o = 16 * (CH * X + SUB * s), pc(X, SUB * s, SUB * s + n)
+        ts(A("NE", a, a + 16 * n), A("D", a, a + 16 * n), A("EC"), OPS.add, A("EC"), OPS.is_equal)
         for p in range(16):
-            mm(pc(X, SUB * s, SUB * s + SUB), A("EPM", 128 * p, 128 * p + 128), A("NE", 16 * a + p, 16 * a + 1024, 16), p == 0, False)
-        mm(pc(X, SUB * s, SUB * s + SUB), A("BC"), A("ONE", 0, SUB), False, True)
+            mm(o, A("EPM", 128 * p, 128 * p + 128), A("NE", a + p, a + 16 * n, 16), p == 0, False)
+        mm(o, A("BC"), A("ONE", 0, n), False, True)
 
     def o1(t, X):
         a = CH * X
-        ts(A("VV", a, a + CH), pc(X, 0, CH), 0.0, OPS.is_ge)
+        act(A("VV", a, a + CH), pc(X, 0, CH), AFT.Sign)
         mm(A("PQ%d" % X, 0, CH), A("TF" if t == 0 else "TL"), A("VV", a, a + CH), True, False)
-        mm(A("PQ%d" % X, 0, CH), A("BQ"), A("ONE"), False, True)
+        mm(A("PQ%d" % X, 0, CH), A("TB" if t == 0 else "TC"), A("ONE"), False, True)
 
     def o5(t, X):
         a = CH * X
@@ -303,64 +318,60 @@ def rank_program(g, core, T, topo):
 
     def tiny(t, X):
         lo, hi = 8 * X, 8 * X + 8
-        ts(A("TI", lo, hi), A("PQ%d" % X, 128, 136), 2048.0, OPS.add)
-        ts(A("TM", lo, hi), A("TI", lo, hi), 16383, OPS.bitwise_and)
-        if t == 0:
-            ts(A("TX", lo, hi), A("TM", lo, hi), 4096.0, OPS.max)
-        else:
-            tt(A("TX", lo, hi), A("TM", lo, hi), A("OLD", lo, hi), OPS.max)
-        ts(A("TU", lo, hi), A("TX", lo, hi), 4095, OPS.bitwise_and)
+        cp(A("TI", lo, hi), A("PQ%d" % X, 128, 136))
+        if t > 0:
+            ts(A("TM", lo, hi), A("TI", lo, hi), 16383, OPS.bitwise_and)
+            tt(A("TI", lo, hi), A("TM", lo, hi), A("TU", lo, hi), OPS.max)
+        ts(A("TU", lo, hi), A("TI", lo, hi), 4095, OPS.bitwise_and)
         ts(A("UL", lo, hi), A("TU", lo, hi), float(OFF), OPS.add)
-        if t < 2:
-            ts(A("OLD", lo, hi), A("TU", lo, hi), 4096.0, OPS.add)
+
+    pend, pcopy = [], []
+
+    def drain(n):
+        for _ in range(min(n, len(pend))):
+            pend.pop(0)()
 
     def fails(w, X):
         lo, hi, a = 8 * X, 8 * X + 8, CH * X
-        ts(A("FA", lo, hi), A("TM", lo, hi), 8192.0, OPS.is_lt, 1792.0, OPS.mult)
-        tt(A("LS", lo, hi), A("FRF", lo, hi), A("FA", lo, hi), OPS.add)
-        cp(A("LSU", lo, hi), A("LS", lo, hi))
-        if w == RO - 1:
-            return
-        mm(A("LQ", a, a + CH), A("IDH"), A("LP", a, a + CH), True, False)
-        for p in range(16):
-            mm(A("LQ", a + 8 * p, a + 8 * p + 8), A("IDH"), A("FA", lo, hi), False, p == 15)
-        cp(A("LU", a, a + CH), A("LQ", a, a + CH))
-        act(I("EW", 3584, "LSU", lo, hi), A("KB"), AFT.Silu)
-        for p in range(16):
-            act(I("FL", 3584, "LU", a + 8 * p, a + 8 * p + 8), A("KA"), AFT.Silu)
+        ts(A("FA", lo, hi), A("TU", lo, hi), 0.0, OPS.is_equal, 1792.0, OPS.mult)
+        if w < RO - 1:
+            mm(A("PR", a, a + CH), A("IDH"), A("LP", a, a + CH), True, False)
+            for p in range(16):
+                mm(A("PR", a + 8 * p, a + 8 * p + 8), A("IDH"), A("FA", lo, hi), False, p == 15)
+            pcopy.append(lambda: cp(A("LU", a, a + CH), A("PR", a, a + CH)))
+            for p in range(16):
+                pend.append(lambda p=p: act(I("FL", 3584, "LU", a + 8 * p, a + 8 * p + 8), A("KA"), AFT.Silu))
+        if X == 1:
+            tt(A("LS"), A("FRF"), A("FA"), OPS.add)
+            cp(A("LSU"), A("LS"))
+            if w < RO - 1:
+                pend.append(lambda: act(I("EW", 3584, "LSU", 0, 16), A("KB"), AFT.Silu))
 
     def nbg(X):
-        a = CH * X
-        ts(A("CB", a, a + CH), I("NW", HALO + NH, "UL", 8 * X, 8 * X + 8), 2048.0, OPS.subtract, 0.0625, OPS.mult)
-        ts(A("CL", a, a + CH), A("CB", a, a + CH), 16.0, OPS.mult, 2048.0 + OFF, OPS.add)
-
-    RN = ("Ra", "Rb", "Rc")
+        a, nb = CH * X, I("NW", HALO + NH, "UL", 8 * X, 8 * X + 8)
+        ts(A("CL", a, a + CH), nb, 2048.0 + OFF, OPS.add)
+        act(A("CB", a, a + CH), nb, AFT.Copy, 0.0, 0.0625)
 
     def rt(t, X):
-        a = CH * X
-        tt(A(RN[t], a, a + CH), pc(X, 0, CH), A("CB", a, a + CH), OPS.min)
+        a, b, r = CH * X, CH * X + CH, ("Ra", "Rb")[t]
+        tt(A(r, a, b), pc(X, 0, CH), A("CB", a, b), OPS.min)
+        act(A(("SA", "SB")[t], a, b), A(r, a, b), AFT.Copy, (-512.0, -256.0)[t])
 
     def relay_a():
         cp(A("Ch"), A("NAU"))
         for h in range(2):
             for k in range(8):
-                mm(A("PT", 32 * k + 16 * h, 32 * k + 16 * h + 16), A("Ch", 128 * h, 128 * h + 128), A("IDH", 16 * k, 16 * k + 16), True, True)
-        cp(A("Th"), A("PT", 0, 256))
+                mm(A("PR", 32 * k + 16 * h, 32 * k + 16 * h + 16), A("Ch", 128 * h, 128 * h + 128), A("IDH", 16 * k, 16 * k + 16), True, True)
 
-    def relay_b():
-        for h in range(8):
+    def relay_b(h0, h1):
+        for h in range(h0, h1):
             for k in range(8):
-                mm(A("LPS", h, 256, 8), A("ZM", 240 * h + 112 - 16 * k, 240 * h + 240 - 16 * k), A("Th", 32 * k, 32 * k + 32), k == 0, k == 7)
-
-    def merge01():
-        ts(A("Ra"), A("Ra"), 512.0, OPS.subtract)
-        ts(A("Rb"), A("Rb"), 256.0, OPS.subtract)
-        tt(A("Ra"), A("Ra"), A("Rb"), OPS.max)
+                mm(A("PR", 256 + h, 512, 8), A("ZM", 240 * h + 112 - 16 * k, 240 * h + 240 - 16 * k), A("Th", 32 * k, 32 * k + 32), k == 0, k == 7)
 
     def decode(w, X):
         a, b = CH * X, CH * X + CH
-        rt(2, X)
-        tt(A("Rc", a, b), A("Rc", a, b), A("Ra", a, b), OPS.max)
+        tt(pc(X, CH, 2 * CH), pc(X, 0, CH), A("CB", a, b), OPS.min)
+        tt(A("Rc", a, b), pc(X, CH, 2 * CH), A("Ra", a, b), OPS.max)
         ts(A("CI", a, b), A("Rc", a, b), 16.0, OPS.mult, 2048.0, OPS.add)
         ts(A("CJ", a, b), A("CI", a, b), 4095, OPS.bitwise_and)
         if w < RO - 1:
@@ -372,10 +383,9 @@ def rank_program(g, core, T, topo):
 
     def update_a():
         xs = A("XR", 0, 4096, 16)
-        tt(A("DX"), I("BW", HALO + NH, "UL", 0, 16), xs, OPS.subtract)
+        tt(A("DX"), I("BW", 4104, "UL", 0, 16), xs, OPS.subtract)
         ts(A("DC"), A("DX"), -2.0, OPS.max, 2.0, OPS.min)
-        tt(A("XN"), A("DC"), xs, OPS.add)
-        cp(I("AW", 3584, "LSU", 0, 16), A("XN"))
+        tt(I("AW", 3584, "LSU", 0, 16), A("DC"), xs, OPS.add)
 
     def parity():
         mm(A("PM", 64, 80), A("OH"), A("FA"), True, True)
@@ -386,60 +396,65 @@ def rank_program(g, core, T, topo):
 
     for w in range(RO):
         last = w == RO - 1
-        cp(A("F", VA, VA + 256), A("LG%d" % w))
-        seeds("v", 0, 0)
-        seeds("s", 0, 1)
-        seeds("v", 1, 0)
-        seeds("s", 1, 1)
+        act(A("F", VA, VA + 256), A("LG%d" % w))
         if not last:
             relay_a()
-        xrep("v", 0)
+        seeds("v", 0, 0)
+        seeds("s", 0, 1)
+        xrep(1)
+        seeds("s", 1, 0)
+        seeds("s", 1, 1)
+        if w == 0:
+            rest()
+        xrep(0)
         slist(0)
-        xrep("s", 1)
         if not last:
-            act(I("FL", 3584, "FRL", 0, 16), A("KC"), AFT.Silu)
-            relay_b()
+            act(A("Th"), A("PR", 0, 256))
+            relay_b(0, 4)
+        if w == 0:
+            op("v", (T.BW[:, 4103:4104], [("BW", 4096, 4104)], []), [], lambda: g.vector.memset(T.BW[:, 4103:4104], 1024.0))
         G(0, 0)
-        slist(1)
         G(0, 1)
+        slist(1)
         H(0, 0)
         H(0, 1)
         if not last:
-            cp(A("LP"), A("LPS", 0, 256))
+            act(I("FL", 3584, "FRL", 0, 16), A("KC"), AFT.Silu)
         if w == 0:
-            ts(A("NW", 8, 8 + OB), A("NT"), 1.0, OPS.add)
-            ts(A("HN"), A("NT", 0, NH), 2047.0, OPS.min, 2049.0, OPS.add)
-            ts(A("HN"), A("HN"), 4095, OPS.bitwise_and)
+            ts(A("HN"), A("NT", 0, NH), 2047.0, OPS.min, 1.0, OPS.add)
             send(prv, HNB, A("HN"), "hn", "lhn")
-            ts(A("NW", 8, 8 + OB), A("NW", 8, 8 + OB), 4095, OPS.bitwise_and)
-        for t in range(3):
-            for X in range(2):
-                if t == 2 and X == 1:
-                    break
-                nX = 1 - X
-                G(nX, 0)
-                o1(t, X)
-                G(nX, 1)
-                o5(t, X)
-                H(nX, 0)
-                H(nX, 1)
-                tiny(t, X)
-                if t < 2:
-                    rt(t, X)
-                    nbg(X)
-                if t == 0:
-                    fails(w, X)
-        merge01()
+            ts(A("NW", 8, 8 + OB), A("NT"), 2047.0, OPS.subtract)
+        for slot in range(5):
+            t, X = slot // 2, slot % 2
+            nX = 1 - X
+            o1(t, X)
+            if slot == 0 and not last:
+                relay_b(4, 8)
+                act(A("LP"), A("PR", 256, 512))
+            G(nX, 0, CH)
+            if pcopy:
+                pcopy.pop(0)()
+            if slot > 0:
+                drain((8, 9, 9, 99)[slot - 1])
+            o5(t, X)
+            H(nX, 0, CH)
+            tiny(t, X)
+            if t < 2:
+                rt(t, X)
+                nbg(X)
+            if t == 0:
+                fails(w, X)
+        o1(2, 1)
+        tt(A("Ra"), A("SA"), A("SB"), OPS.max)
         decode(w, 0)
         if not last:
             extract(w + 1)
         decode(w, 1)
         if not last:
             ghosts_out(w + 1)
-            select_a(w + 1)
+            select_a()
         else:
             dma("y", T.yf[:], T.YW[:, 0:VA], [("YW", 0, VA)], [], "oy")
-        o1(2, 1)
         o5(2, 1)
         if not last:
             parity()
@@ -447,11 +462,11 @@ def rank_program(g, core, T, topo):
         update_a()
         if last:
             dma("y", T.ya[:], T.AW[:, 0:VA], [("AW", 0, VA)], [], "oa")
-        elif w == RO - 2:
-            ts(A("YT"), A("F", 0, VA), 1.0, OPS.subtract)
-            ts(A("YT"), A("YT"), 4095, OPS.bitwise_and)
-            cp(A("YW", 0, VA), A("YT"))
-        if not last:
+        else:
+            if w == RO - 2:
+                ts(A("YT"), A("F", 0, VA), 1.0, OPS.subtract)
+                ts(A("YT"), A("YT"), 4095, OPS.bitwise_and)
+                cp(A("YW", 0, VA), A("YT"))
             select_b()
 
     need("y", "oy", 16)

from concourse.mybir import AluOpType as OPS, ActivationFunctionType as AFT, AxisListType

VA, OB, CAP, S, RO = 1280, 2048, 256, 272, 6
CH, SUB = 128, 64
OFF = 7
HALO = OB + 1 + OFF
NH = 2047
C4 = 1.5 * 2.0 ** 26
C3 = C4 + 8.0

DTS = {"b": "bfloat16", "f": "float32", "h": "float16", "i": "int32", "u": "uint16"}
BUFS = """AW3584b BW4104b NW4104f NT2048i HN2047f NA1792i F1792f FI272i BDI16i BDU16u IND320b FL3584f EW3584f FR2560f
IDT1280f PAD256f TN80f FC80f ECW80f EL80f CU80f WT80f PP80f OFS80f OU80u ZZ80f FH256h FRL16u FRF16f NAU256u Ch256h Th256h
LP256h LU256u SG4096h CB256f CL256u XR4096b D4096b NE4096b VV256b SC256h SA256f SB256f Ra256f Rb256f Rc256f TI16i TM16i
TU16i UL16u FA16h LS16f LSU16u ES1f EI1i EO1i EC1f DX256b DC256b CI256i CJ256i GS256h YW1792f YT1280i IP1i LPI1i
GPI1i PCF1f LPC1f GPC1f QE1f LM128f GM128f CM128f SAM128b SGL128b IDM128f IDH128h IDL128b TRI128f LTM128f WK128f TF128b
TL128b TB128b TC128b BC128b BR128f ONE128b OH128h XL240f HE8f GE8f ZT240f ZM1920h EPM2048b ELM2048h DPM2048h KA128f
KB256f KC256f"""
SCRATCH = {}
for _b in BUFS.split():
    _n = _b.rstrip("bfhiu").rstrip("0123456789")
    SCRATCH[_n] = ("sbuf", [128, int(_b[len(_n):-1])], DTS[_b[-1]])
for _w in range(RO):
    SCRATCH["LG%d" % _w] = ("sbuf", [128, 256], "float16")
PS = ("PC0", "PC1", "PQ0", "PQ1", "PR", "PM")
for _n in PS:
    SCRATCH[_n] = ("psum", [128, 512], "float32")
LOADS = ["f0", "nba", "xa", "xb", "bd", "nbb"]
SEMAPHORES = (["cv", "cs", "cp", "cg", "hb", "hn", "lhb", "lhn", "oy", "oa"] + ["ld_" + n for n in LOADS]
              + [k + str(w) for k in ("gh", "lg", "xf", "xe") for w in range(RO)])


def rank_program(g, core, T, topo):
    rank = T.rank_of(core)
    if rank is None:
        return
    nxt, prv = T.cores[(rank + 1) % 4], T.cores[(rank + 3) % 4]
    Q = {"v": g.vector, "s": g.scalar, "p": g.tensor, "g": g, "y": g.sync}
    CS = {"v": "cv", "s": "cs", "p": "cp", "g": "cg"}
    cnt = {"cv": 0, "cs": 0, "cp": 0, "cg": 0}
    known = {q: {} for q in Q}
    clocks = {}
    acc = {}

    def need(q, sem, val):
        if known[q].get(sem, 0) >= val:
            return
        Q[q].wait_ge(T.sem[sem], val)
        known[q][sem] = val
        for s2, v2 in clocks.get((sem, val), {}).items():
            if known[q].get(s2, 0) < v2:
                known[q][s2] = v2

    def deps(q, reads, writes):
        want = {}
        for lst, isw in ((reads, False), (writes, True)):
            for name, lo, hi in lst:
                ps = name in PS
                for a in acc.get(name, []):
                    if not ps and (a[1] <= lo or hi <= a[0]):
                        continue
                    if ps and a[2] == q and (q == "p" or not a[5]) or not (isw or a[5] or ps):
                        continue
                    if want.get(a[3], 0) < a[4]:
                        want[a[3]] = a[4]
        for sem in sorted(want):
            need(q, sem, want[sem])

    def note(q, reads, writes, sem, val):
        c = dict(known[q])
        c[sem] = val
        clocks[(sem, val)] = c
        for lst, isw in ((reads, False), (writes, True)):
            for name, lo, hi in lst:
                l = acc.setdefault(name, [])
                if isw or name in PS:
                    l[:] = [a for a in l if not (name in PS or (lo <= a[0] and a[1] <= hi))]
                else:
                    l[:] = [a for a in l if a[5] or a[2] != q or a[3] != sem or not (lo <= a[0] and a[1] <= hi)]
                l.append([lo, hi, q, sem, val, isw])

    def A(name, lo=0, hi=None, st=1):
        if hi is None:
            hi = T[name].shape[1]
        ap = T[name][:, lo:hi] if st == 1 else T[name][:, lo:hi:st]
        return (ap, [(name, lo, hi)], [])

    def I(win, w, off, o0, o1):
        return (T[win][:, 0:w].indirect(T[off][:, o0:o1]), [(win, 0, w)], [(off, o0, o1)])

    def op(q, out, ins, call):
        reads = list(out[2])
        for x in ins:
            reads += x[1] + x[2]
        deps(q, reads, out[1])
        sem = CS[q]
        cnt[sem] += 1
        call().then_inc(T.sem[sem], 1)
        note(q, reads, out[1], sem, cnt[sem])

    def u(x):
        return x[0] if isinstance(x, tuple) else x

    def cp(out, in_):
        op("v", out, [in_], lambda: g.vector.tensor_copy(out=out[0], in_=in_[0]))

    def tt(out, a, b, o):
        op("v", out, [a, b], lambda: g.vector.tensor_tensor(out=out[0], in0=a[0], in1=b[0], op=o))

    def ts(out, a, s1, o0, s2=None, o1=None):
        ins = [a] + [x for x in (s1, s2) if isinstance(x, tuple)]
        if o1 is None:
            op("v", out, ins, lambda: g.vector.tensor_scalar(out=out[0], in0=a[0], scalar1=u(s1), scalar2=None, op0=o0))
        else:
            op("v", out, ins, lambda: g.vector.tensor_scalar(out=out[0], in0=a[0], scalar1=u(s1), scalar2=u(s2), op0=o0, op1=o1))

    def ms(out, c):
        op("v", out, [], lambda: g.vector.memset(out[0], c))

    def act(out, in_, f=AFT.Copy, bias=0.0, scale=1.0):
        if bias == 0.0 and scale == 1.0:
            op("s", out, [in_], lambda: g.scalar.activation(out=out[0], in_=in_[0], func=f))
        else:
            op("s", out, [in_], lambda: g.scalar.activation(out=out[0], in_=in_[0], func=f, bias=bias, scale=scale))

    def mm(out, lhsT, rhs, st, sp):
        op("p", out, [lhsT, rhs], lambda: g.tensor.matmul(out=out[0], lhsT=lhsT[0], rhs=rhs[0], start=st, stop=sp))

    def io(out, pat, base, cm=0, small=True):
        if small:
            op("g", out, [], lambda: g.iota(out[0], pat, base, cm, allow_small_or_imprecise_dtypes=True))
        else:
            op("g", out, [], lambda: g.iota(out[0], pat, base, cm))

    def gcopy(out, in_, n):
        op("g", out, [in_], lambda: g.affine_select(out[0], in_[0], [[0, n]], OPS.is_gt, 0.0, 1, 0))

    def dma(q, out_ap, in_ap, reads, writes, sem):
        deps(q, reads, writes)
        Q[q].dma_start(out=out_ap, in_=in_ap).then_inc(T.sem[sem], 16)
        note(q, reads, writes, sem, 16)

    def send(dst, outp, inp, rsem, lsem):
        deps("g", inp[1], [])
        rid, pid, _ = topo.addr(dst)
        g.remote_dma(out_ap=outp[0], in_ap=inp[0], remote_sem=T.sem[rsem], local_sem=T.sem[lsem], pid=pid, routing_id=rid,
                     dma_engine_mask=topo.mask(core, dst))
        note("g", inp[1], [], lsem, len(topo.engines(core, dst)))

    def arrive(src, outp, rsem):
        acc.setdefault(outp[1][0][0], []).append([outp[1][0][1], outp[1][0][2], "r", rsem, len(topo.engines(src, core)), True])

    dma("s", T.FI[:], T.f0[:], [], [("FI", 0, S)], "ld_f0")
    dma("s", T.BW[:, 8:8 + OB], T.xb[:], [], [("BW", 8, 8 + OB)], "ld_xb")
    dma("y", T.BDI[:], T.bd[:], [], [("BDI", 0, 16)], "ld_bd")
    dma("y", T.NA[:, 0:VA], T.nba[:], [], [("NA", 0, VA)], "ld_nba")
    dma("s", T.AW[:, 0:VA], T.xa[:], [], [("AW", 0, VA)], "ld_xa")
    HB, HNB = A("BW", HALO, HALO + NH), A("NW", HALO, HALO + NH)
    arrive(nxt, HB, "hb")
    arrive(nxt, HNB, "hn")
    for w in range(RO):
        arrive(prv, A("LG%d" % w), "gh%d" % w)

    io(A("IP"), [[0, 1]], 0, 1, False)
    io(A("LM"), [[0, 8], [1, 16]], 1)
    io(A("GM"), [[1, 8], [0, 16]], 0)
    io(A("CM"), [[1, 128]], 0)
    io(A("TN"), [[1, 80]], VA)
    io(A("PAD"), [[1, CAP]], 1536 + 64)
    io(A("IDT"), [[1, 80], [80, 16]], 64)
    io(A("NA", VA, 1792), [[1, 512]], VA, 0, False)
    io(A("XL"), [[1, 240]], -112)
    io(A("HE"), [[1, 8]], 0)
    send(prv, HB, A("BW", 8, 8 + NH), "hb", "lhb")
    need("y", "lhb", len(topo.engines(core, prv)))
    dma("y", T.NT[:], T.nbb[:], [], [("NT", 0, OB)], "ld_nbb")
    ms(A("FL", 0, VA), 33.0)
    ms(A("EW", S, VA), 0.0)
    ms(A("F", S, 1792), 0.0)
    ms(A("ZZ"), 0.0)
    ms(A("KB"), 64.0)
    ms(A("KA"), 33.0)
    ms(A("KC"), 0.0)
    ts(A("LPI"), A("IP"), 15, OPS.bitwise_and)
    ts(A("GPI"), A("IP"), 4, OPS.arith_shift_right)
    cp(A("PCF"), A("IP"))
    ts(A("LPC"), A("LPI"), 1.0, OPS.add)
    cp(A("GPC"), A("GPI"))
    ts(A("QE"), A("LPI"), 80.0, OPS.mult)
    ts(A("TN"), A("TN"), A("QE"), OPS.add)
    ts(A("SAM"), A("GM"), A("GPC"), OPS.is_equal)
    ts(A("FI"), A("FI"), 1.0, OPS.add)
    ts(A("IDM"), A("CM"), A("PCF"), OPS.is_equal)
    ts(A("FI"), A("FI"), 4095, OPS.bitwise_and)
    ts(A("WK"), A("LM"), A("LPC"), OPS.is_gt)
    cp(A("F", 0, S), A("FI"))
    tt(A("TRI"), A("WK"), A("SAM"), OPS.mult)
    ts(A("IND"), A("F", 0, 320), 0.0, OPS.is_gt)
    tt(A("SGL"), A("SAM"), A("LM"), OPS.mult)
    for q in range(4):
        ts(A("EPM", 128 * q, 128 * q + 128), A("SGL"), float(q + 1), OPS.is_equal, 1024.0, OPS.mult)
        mm(A("PM", 0, 80), A("EPM", 128 * q, 128 * q + 128), A("IND", 80 * q, 80 * q + 80), q == 0, q == 3)
    ms(A("FC"), 33.0)
    tt(A("IDL"), A("IDM"), A("LM"), OPS.mult)
    ts(A("ECW"), A("PM", 0, 80), 0.5, OPS.is_gt, 64.0, OPS.mult)

    def ghosts_out(w):
        act(A("GS"), I("F", VA, "BDU", 0, 16), AFT.Relu, -2048.0)
        send(nxt, A("LG%d" % w), A("GS"), "gh%d" % w, "lg%d" % w)

    def extract(w):
        dma("y", T.ECW[:], T.EW[0:128:16, 0:VA], [("EW", 0, VA)], [("ECW", 0, 80)], "xe%d" % w)
        dma("y", T.FC[:], T.FL[0:128:16, 0:VA], [("FL", 0, VA)], [("FC", 0, 80)], "xf%d" % w)

    def select_a():
        tt(A("EL"), A("FC"), A("ECW"), OPS.is_gt)
        op("v", A("CU"), [A("EL"), A("ZZ")], lambda: g.vector.tensor_tensor_scan(
            out=T.CU[:], data0=T.EL[:], data1=T.ZZ[:], initial=0.0, op0=OPS.add, op1=OPS.add))
        mm(A("PM", 0, 1), A("TRI"), A("CU", 79, 80), True, True)
        ts(A("WT"), A("EL"), -4096.0, OPS.mult)
        tt(A("WT"), A("WT"), A("TN"), OPS.add)
        ts(A("PP"), A("CU"), A("PM", 0, 1), OPS.add, 1.0, OPS.subtract)
        tt(A("OFS"), A("WT"), A("PP"), OPS.max)
        cp(A("OU"), A("OFS"))
        act(A("FR", 0, CAP), A("PAD"))
        act(I("FR", 2560, "OU", 0, 80), A("IDT"), AFT.Silu)

    def select_b():
        act(A("FH"), A("FR", 0, CAP))
        for l in range(16):
            mm(A("PM", 16, 32), A("DPM", 128 * l, 128 * l + 128), A("FH", l, CAP, 16), l == 0, l == 15)
        ts(A("FRL"), A("PM", 16, 32), 64.0, OPS.subtract)
        cp(A("NAU"), I("NA", 1792, "FRL", 0, 16))
        ts(A("FRF"), A("PM", 16, 32), 64.0, OPS.subtract)

    select_a()
    cp(A("BDU"), A("BDI"))
    ghosts_out(0)
    mm(A("PM", 128, 128 + S), A("SAM"), A("IND", 0, S), True, True)
    ts(A("EW", 0, S), A("PM", 128, 128 + S), 0.5, OPS.is_gt, 64.0, OPS.mult)
    for p in range(16):
        ts(A("DPM", 128 * p, 128 * p + 128), A("IDL"), float(p + 1), OPS.is_equal)
    ms(A("BW", 0, 8), 1024.0)
    ms(A("NW", 0, 8), -2048.0)
    ms(A("AW", VA, 1792), 0.0)
    ms(A("EC"), C3)
    for p in range(4, 16):
        ts(A("EPM", 128 * p, 128 * p + 128), A("SGL"), float(p + 1), OPS.is_equal, 1024.0, OPS.mult)
    cp(A("IDH"), A("IDM"))
    ts(A("BR"), A("IDM"), -128.0, OPS.mult)
    ms(A("ONE"), 1.0)
    ts(A("WK"), A("LM"), A("LPC"), OPS.is_lt)
    tt(A("LTM"), A("WK"), A("SAM"), OPS.mult)
    for m, o, b in (("TRI", "TF", "TB"), ("LTM", "TL", "TC")):
        tt(A("WK"), A("IDM"), A(m), OPS.subtract)
        ts(A(o), A("WK"), 512.0, OPS.mult)
        ts(A(b), A(m), -512.0, OPS.mult)
        tt(A(b), A(b), A("BR"), OPS.add)
    select_b()

    def rest():
        for p in range(16):
            ts(A("ELM", 128 * p, 128 * p + 128), A("SGL"), float(p + 1), OPS.is_equal, 16.0, OPS.mult)
        ts(A("OH"), A("ONE"), 1.0 / 256.0, OPS.mult)
        ts(A("BC"), A("ONE"), -109.0, OPS.mult)
        ts(A("ZT"), A("XL"), 1.0, OPS.add, A("LPC"), OPS.is_equal)
        ts(A("GE"), A("HE"), A("GPC"), OPS.is_equal)
        for h in range(8):
            ts(A("ZM", 240 * h, 240 * h + 240), A("ZT"), A("GE", h, h + 1), OPS.mult)

    def pc(X, lo, hi):
        return A("PC%d" % X, lo, hi)

    def seeds(q, X, s):
        a = CH * X + SUB * s
        if q == "v":
            ts(A("SG", 16 * a, 16 * a + 1024), I("F", 1792, "NAU", a, a + SUB), 2048.0, OPS.subtract, 0.0625, OPS.mult)
        else:
            act(A("SG", 16 * a, 16 * a + 1024), I("F", 1792, "NAU", a, a + SUB), AFT.Copy, -128.0, 0.0625)
        for p in range(16):
            mm(pc(X, SUB * s, SUB * s + SUB), A("DPM", 128 * p, 128 * p + 128), A("SG", 16 * a + p, 16 * a + 1024, 16), p == 0, p == 15)

    def slist(X):
        ts(A("CL", CH * X, CH * X + CH), pc(X, 0, CH), 16.0, OPS.mult, 2048.0 + OFF, OPS.add)
        act(A("CB", CH * X, CH * X + CH), pc(X, 0, CH))

    def xrep(X):
        a, b = 16 * CH * X, 16 * CH * X + 16 * CH
        (act if X else cp)(A("XR", a, b, 16), I("AW", 1792, "FRL", 8 * X, 8 * X + 8))
        for k, n in ((8, 128), (4, 256), (2, 512), (1, 1024)):
            if X:
                gcopy(A("XR", a + k, b, 2 * k), A("XR", a, b, 2 * k), n)
            else:
                cp(A("XR", a + k, b, 2 * k), A("XR", a, b, 2 * k))

    def G(X, s, n=SUB):
        a = 16 * (CH * X + SUB * s)
        tt(A("D", a, a + 16 * n), I("BW", 4104, "CL", a // 16, a // 16 + n), A("XR", a, a + 16 * n), OPS.subtract)

    def H(X, s, n=SUB):
        a, o = 16 * (CH * X + SUB * s), pc(X, SUB * s, SUB * s + n)
        ts(A("NE", a, a + 16 * n), A("D", a, a + 16 * n), A("EC"), OPS.add, A("EC"), OPS.is_equal)
        for p in range(16):
            mm(o, A("EPM", 128 * p, 128 * p + 128), A("NE", a + p, a + 16 * n, 16), p == 0, False)
        mm(o, A("BC"), A("ONE", 0, n), False, True)

    def o1(t, X):
        a = CH * X
        act(A("VV", a, a + CH), pc(X, 0, CH), AFT.Sign)
        mm(A("PQ%d" % X, 0, CH), A("TF" if t == 0 else "TL"), A("VV", a, a + CH), True, False)
        mm(A("PQ%d" % X, 0, CH), A("TB" if t == 0 else "TC"), A("ONE"), False, True)

    def o5(t, X):
        a = CH * X
        tt(A("SC", a, a + CH), A("PQ%d" % X, 0, CH), A("CB", a, a + CH), OPS.min)
        for l in range(16):
            mm(A("PQ%d" % X, 128, 136), A("ELM", 128 * l, 128 * l + 128), A("SC", a + l, a + CH, 16), l == 0, l == 15)

    def tiny(t, X):
        lo, hi = 8 * X, 8 * X + 8
        cp(A("TI", lo, hi), A("PQ%d" % X, 128, 136))
        if t > 0:
            ts(A("TM", lo, hi), A("TI", lo, hi), 16383, OPS.bitwise_and)
            tt(A("TI", lo, hi), A("TM", lo, hi), A("TU", lo, hi), OPS.max)
        ts(A("TU", lo, hi), A("TI", lo, hi), 4095, OPS.bitwise_and)
        ts(A("UL", lo, hi), A("TU", lo, hi), float(OFF), OPS.add)

    pend, pcopy = [], []

    def drain(n):
        for _ in range(min(n, len(pend))):
            pend.pop(0)()

    def fails(w, X):
        lo, hi, a = 8 * X, 8 * X + 8, CH * X
        ts(A("FA", lo, hi), A("TU", lo, hi), 0.0, OPS.is_equal, 1792.0, OPS.mult)
        if w < RO - 1:
            mm(A("PR", a, a + CH), A("IDH"), A("LP", a, a + CH), True, False)
            for p in range(16):
                mm(A("PR", a + 8 * p, a + 8 * p + 8), A("IDH"), A("FA", lo, hi), False, p == 15)
            pcopy.append(lambda: cp(A("LU", a, a + CH), A("PR", a, a + CH)))
            for p in range(16):
                pend.append(lambda p=p: act(I("FL", 3584, "LU", a + 8 * p, a + 8 * p + 8), A("KA"), AFT.Silu))
        if X == 1:
            tt(A("LS"), A("FRF"), A("FA"), OPS.add)
            cp(A("LSU"), A("LS"))
            if w < RO - 1:
                pend.append(lambda: act(I("EW", 3584, "LSU", 0, 16), A("KB"), AFT.Silu))

    def nbg(X):
        a, nb = CH * X, I("NW", HALO + NH, "UL", 8 * X, 8 * X + 8)
        ts(A("CL", a, a + CH), nb, 2048.0 + OFF, OPS.add)
        act(A("CB", a, a + CH), nb, AFT.Copy, 0.0, 0.0625)

    def rt(t, X):
        a, b, r = CH * X, CH * X + CH, ("Ra", "Rb")[t]
        tt(A(r, a, b), pc(X, 0, CH), A("CB", a, b), OPS.min)
        act(A(("SA", "SB")[t], a, b), A(r, a, b), AFT.Copy, (-512.0, -256.0)[t])

    def relay_a():
        cp(A("Ch"), A("NAU"))
        for h in range(2):
            for k in range(8):
                mm(A("PR", 32 * k + 16 * h, 32 * k + 16 * h + 16), A("Ch", 128 * h, 128 * h + 128), A("IDH", 16 * k, 16 * k + 16), True, True)

    def relay_b(h0, h1):
        for h in range(h0, h1):
            for k in range(8):
                mm(A("PR", 256 + h, 512, 8), A("ZM", 240 * h + 112 - 16 * k, 240 * h + 240 - 16 * k), A("Th", 32 * k, 32 * k + 32), k == 0, k == 7)

    def decode(w, X):
        a, b = CH * X, CH * X + CH
        tt(pc(X, CH, 2 * CH), pc(X, 0, CH), A("CB", a, b), OPS.min)
        tt(A("Rc", a, b), pc(X, CH, 2 * CH), A("Ra", a, b), OPS.max)
        ts(A("CI", a, b), A("Rc", a, b), 16.0, OPS.mult, 2048.0, OPS.add)
        ts(A("CJ", a, b), A("CI", a, b), 4095, OPS.bitwise_and)
        if w < RO - 1:
            cp(I("F", 1792, "FRL", 8 * X, 8 * X + 8), A("CJ", a, b))
        else:
            ts(A("CI", a, b), A("CJ", a, b), 1.0, OPS.subtract)
            ts(A("CJ", a, b), A("CI", a, b), 4095, OPS.bitwise_and)
            cp(I("YW", 1792, "FRL", 8 * X, 8 * X + 8), A("CJ", a, b))

    def update_a():
        xs = A("XR", 0, 4096, 16)
        tt(A("DX"), I("BW", 4104, "UL", 0, 16), xs, OPS.subtract)
        ts(A("DC"), A("DX"), -2.0, OPS.max, 2.0, OPS.min)
        tt(I("AW", 3584, "LSU", 0, 16), A("DC"), xs, OPS.add)

    def parity():
        mm(A("PM", 64, 80), A("OH"), A("FA"), True, True)
        op("v", A("ES"), [A("PM", 64, 80)], lambda: g.vector.tensor_reduce(out=T.ES[:], in_=T.PM[:, 64:80], axis=AxisListType.X, op=OPS.add))
        cp(A("EI"), A("ES"))
        ts(A("EO"), A("EI"), 1, OPS.bitwise_and)
        ts(A("EC"), A("EO"), -8.0, OPS.mult, C3, OPS.add)

    for w in range(RO):
        last = w == RO - 1
        act(A("F", VA, VA + 256), A("LG%d" % w))
        if not last:
            relay_a()
        seeds("v", 0, 0)
        seeds("s", 0, 1)
        xrep(1)
        seeds("s", 1, 0)
        seeds("s", 1, 1)
        if w == 0:
            rest()
        xrep(0)
        slist(0)
        if not last:
            act(A("Th"), A("PR", 0, 256))
            relay_b(0, 4)
        if w == 0:
            op("v", (T.BW[:, 4103:4104], [("BW", 4096, 4104)], []), [], lambda: g.vector.memset(T.BW[:, 4103:4104], 1024.0))
        G(0, 0)
        G(0, 1)
        slist(1)
        H(0, 0)
        H(0, 1)
        if not last:
            act(I("FL", 3584, "FRL", 0, 16), A("KC"), AFT.Silu)
        if w == 0:
            ts(A("HN"), A("NT", 0, NH), 2047.0, OPS.min, 1.0, OPS.add)
            send(prv, HNB, A("HN"), "hn", "lhn")
            ts(A("NW", 8, 8 + OB), A("NT"), 2047.0, OPS.subtract)
        for slot in range(5):
            t, X = slot // 2, slot % 2
            nX = 1 - X
            o1(t, X)
            if slot == 0 and not last:
                relay_b(4, 8)
                act(A("LP"), A("PR", 256, 512))
            G(nX, 0, CH)
            if pcopy:
                pcopy.pop(0)()
            if slot > 0:
                drain((8, 9, 9, 99)[slot - 1])
            o5(t, X)
            H(nX, 0, CH)
            tiny(t, X)
            if t < 2:
                rt(t, X)
                nbg(X)
            if t == 0:
                fails(w, X)
        o1(2, 1)
        tt(A("Ra"), A("SA"), A("SB"), OPS.max)
        decode(w, 0)
        if not last:
            extract(w + 1)
        decode(w, 1)
        if not last:
            ghosts_out(w + 1)
            select_a()
        else:
            dma("y", T.yf[:], T.YW[:, 0:VA], [("YW", 0, VA)], [], "oy")
        o5(2, 1)
        if not last:
            parity()
        tiny(2, 1)
        update_a()
        if last:
            dma("y", T.ya[:], T.AW[:, 0:VA], [("AW", 0, VA)], [], "oa")
        else:
            if w == RO - 2:
                ts(A("YT"), A("F", 0, VA), 1.0, OPS.subtract)
                ts(A("YT"), A("YT"), 4095, OPS.bitwise_and)
                cp(A("YW", 0, VA), A("YT"))
            select_b()

    need("y", "oy", 16)
    need("y", "oa", 16)
    for w in range(RO):
        need("g", "lg%d" % w, 16)
    need("g", "lhb", 16)
    need("g", "lhn", 16)
    for s in ("cv", "cs", "cp", "cg"):
        need("y", s, cnt[s])
